import numpy as np
import ml_dtypes


def mxq(x, axis, fmt="e4m3"):
    dtype, down = {"e4m3": (ml_dtypes.float8_e4m3fn, 7), "e5m2": (ml_dtypes.float8_e5m2, 14)}[fmt]
    v = np.moveaxis(np.asarray(x, np.float32).astype(ml_dtypes.bfloat16).astype(np.float64), axis, -1)
    blocks = v.reshape(v.shape[:-1] + (-1, 32))
    amax = np.abs(blocks).max(-1, keepdims=True)
    byte = np.maximum(np.where(amax > 0, np.frexp(amax)[1] - 1 + 127, 0) - down, 1)
    scale = np.exp2(byte - 127.0)
    codes = (blocks / scale).astype(np.float32).astype(dtype).astype(np.float64)
    return np.moveaxis((codes * scale).reshape(v.shape), -1, axis)


WIDE = False


def mx_kscale(k):
    if not WIDE:
        return np.ones(k)
    levels = np.array([10, -10, 5, -5, 0])
    if k % 512:
        return np.exp2(np.random.permutation(np.resize(levels, k // 32))).repeat(32)
    a = np.empty((k // 512, 16))
    for p in range(k // 512):
        a[p, :8] = np.random.permutation(np.resize(levels, 8))
        for g in range(8):
            far = levels[np.abs(levels - a[p, g]) >= 10]
            a[p, g + 8] = far[np.random.randint(len(far))]
    return np.exp2(a.ravel()).repeat(32)


def f64(x):
    return np.asarray(x).astype(np.float64)


def striped(idx):
    return np.tile(idx.reshape(-1, 16).T, (8, 1)).astype(np.uint16)


def unstriped(offs):
    return offs[:16].T.reshape(-1).astype(np.int64)


def pack_weight(w):
    k, n = w.shape
    w = f64(np.asarray(w, np.float32).astype(ml_dtypes.bfloat16)).reshape(k // 32, 32, n)
    amax = np.abs(w).max(1)
    byte = np.clip(np.where(amax > 0, np.frexp(amax)[1] - 1 + 127 - 7, 1), 1, 254)
    scaled = (w * np.exp2(127.0 - byte)[:, None, :]).reshape(k, n).astype(np.float32)
    words = np.ascontiguousarray(scaled.reshape(k // 512, 128, 4, n).transpose(0, 1, 3, 2)).astype(ml_dtypes.float8_e4m3fn).view(np.uint8)
    return words, np.ascontiguousarray(byte.astype(np.uint8).reshape(k // 512, 16, n))


def unpack_weight(words, scales):
    g, p, n, _ = words.shape
    vals = np.ascontiguousarray(words).view(ml_dtypes.float8_e4m3fn).astype(np.float64) * np.repeat(np.exp2(scales.astype(np.float64) - 127.0), 8, axis=1)[..., None]
    return vals.transpose(0, 1, 3, 2).reshape(g * 512, n)


K, T, D, S, V, N = 512, 2048, 4, 512, 256, 256


def setup_inputs():
    n = np.random.standard_normal
    s = mx_kscale(K)[:, None]
    words, scales = pack_weight(n((K, N)) / np.sqrt(K) / s)
    return {
        "xT": (n((K, T)) * s).astype(np.float32),
        "w_words": words,
        "w_scales": scales,
        "gate": np.tile(np.random.uniform(0.2, 1.0, (D, 1, V)) / np.sqrt(D), (1, N, 1)).astype(np.float32),
        "offs": striped(np.random.permutation(T)[:S]),
        "pos1": striped(np.random.permutation(S)[:V]),
        "pos2": striped(np.random.permutation(S)[:V]),
        "pos3": striped(np.random.permutation(S)[:V]),
        "pos4": striped(np.random.permutation(S)[:V]),
    }


def reference(xT, w_words, w_scales, gate, offs, pos1, pos2, pos3, pos4):
    w = unpack_weight(w_words, w_scales)
    idx = unstriped(offs)
    xq = mxq(f64(xT)[:, idx], 0, "e4m3")
    y = w.T @ xq
    return sum(f64(gate[d]) * y[:, unstriped(p)] for d, p in enumerate((pos1, pos2, pos3, pos4)))

@@ -1,0 +1,105 @@
+from contextlib import ExitStack
+
+import concourse.mybir as mybir
+
+F32 = mybir.dt.float32
+BF16 = mybir.dt.bfloat16
+I32 = mybir.dt.int32
+U32 = mybir.dt.uint32
+U16 = mybir.dt.uint16
+U8 = mybir.dt.uint8
+FP8X4 = mybir.dt.float8_e4m3fn_x4
+MULT = mybir.AluOpType.mult
+ADD = mybir.AluOpType.add
+
+P = 128
+PACK = 4
+K, T, S, D, V, N = 512, 2048, 512, 4, 256, 256
+HALF = S // 2
+FLOPS = 2 * K * S * N + 2 * D * N * V
+
+
+def tile_picked_sub_lin_none_sub_e_kernel(tc, xT, w_words, w_scales, gate, offs, pos1, pos2, pos3, pos4, out):
+    nc = tc.nc
+    with ExitStack() as ctx:
+        keep = ctx.enter_context(tc.tile_pool(name="keep", bufs=1))
+        psum = ctx.enter_context(tc.psum_pool(name="psum", bufs=1))
+
+        offs_t = keep.tile([P, S // 16], U16, name="offs_t")
+        pos_t = [keep.tile([P, V // 16], U16, name=f"pos_t{d}") for d in range(D)]
+        planes = [keep.tile([P, T], F32, name=f"plane{t}") for t in range(PACK)]
+        w_codes = keep.tile([P, N], U32, name="w_codes", align_bytes=64)
+        w_bytes = keep.tile([P, N], U8, name="w_bytes", align_bytes=64)
+        gates = [keep.tile([P, D, V], F32, name=f"gates{m}") for m in range(N // P)]
+        picked = keep.tile([P, S, PACK], BF16, name="picked", align_bytes=64)
+        x_codes = [keep.tile([P, HALF], U32, name=f"x_codes{h}", align_bytes=64) for h in range(2)]
+        x_bytes = [keep.tile([P, HALF], U8, name=f"x_bytes{h}", align_bytes=64) for h in range(2)]
+        y = [keep.tile([P, S], F32, name=f"y{m}") for m in range(N // P)]
+        prod = [keep.tile([P, D, V], F32, name=f"prod{m}") for m in range(N // P)]
+        pair = keep.tile([P, 2, V], F32, name="pair")
+        part = [keep.tile([P, V], F32, name=f"part{i}") for i in range(2)]
+        result = [keep.tile([P, V], F32, name=f"result{m}") for m in range(N // P)]
+        warm = keep.tile([P, 2], F32, name="warm")
+
+        nc.sync.dma_start(offs_t[:], offs)
+        x_rows = xT.rearrange("(p t) n -> p t n", t=PACK)
+        for t in range(PACK):
+            nc.sync.dma_start(planes[t][:], x_rows[:, t, :])
+        nc.sync.dma_start(w_codes[:].bitcast(I32), w_words[0].rearrange("p n r -> p (n r)").bitcast(I32))
+        nc.sync.dma_start(gates[0][:], gate[:, 0:P, :].rearrange("d p v -> p d v"))
+        for tile, source in zip(pos_t, (pos1, pos2, pos3, pos4)):
+            nc.sync.dma_start(tile[:], source)
+        nc.sync.dma_start(gates[1][:], gate[:, P : 2 * P, :].rearrange("d p v -> p d v"))
+
+        nc.vector.memset(w_bytes[:].bitcast(I32), 0)
+        for q in range(4):
+            nc.gpsimd.dma_start(w_bytes[32 * q : 32 * q + 4, :].bitcast(I32), w_scales[0, 4 * q : 4 * q + 4, :].bitcast(I32))
+        nc.vector.memset(warm[:], 0.0)
+        nc.scalar.copy(warm[:, 0:1], warm[:, 1:2])
+
+        for t in range(PACK - 1):
+            nc.vector.tensor_copy(picked[:, :, t], planes[t][:].indirect(offs_t[:]))
+        for h in range(2):
+            cols = slice(h * HALF, (h + 1) * HALF)
+            nc.vector.tensor_copy(picked[:, cols, PACK - 1], planes[PACK - 1][:].indirect(offs_t[:, h * 16 : (h + 1) * 16]))
+        for h in range(2):
+            cols = slice(h * HALF, (h + 1) * HALF)
+            nc.vector.quantize_mx(
+                out=x_codes[h][:].bitcast(FP8X4), scales=x_bytes[h][:], in_=picked[:, cols, :].rearrange("p n t -> p (n t)")
+            )
+
+        for h in range(2):
+            for m in range(N // P):
+                rows = slice(m * P, (m + 1) * P)
+                acc = psum.tile([P, HALF], F32, name=f"acc{h}{m}")
+                nc.tensor.matmul_mx(
+                    out=acc[:],
+                    lhsT=w_codes[:, rows].bitcast(FP8X4),
+                    lhsT_scale=w_bytes[:, rows],
+                    rhs=x_codes[h][:].bitcast(FP8X4),
+                    rhs_scale=x_bytes[h][:],
+                    start=True,
+                    stop=True,
+                )
+                dst = y[m][:, h * HALF : (h + 1) * HALF]
+                if h == 0 and m == 0:
+                    nc.vector.tensor_copy(dst, acc[:])
+                else:
+                    nc.scalar.copy(dst, acc[:])
+
+        def fetch(m, d):
+            nc.vector.tensor_tensor(prod[m][:, d, :], y[m][:].indirect(pos_t[d][:]), gates[m][:, d, :], MULT)
+
+        for d in range(D):
+            fetch(0, d)
+        fetch(1, 0)
+        nc.vector.tensor_tensor(pair[:], prod[0][:, 0:2, :], prod[0][:, 2:4, :], ADD)
+        fetch(1, 1)
+        fetch(1, 2)
+        nc.vector.tensor_tensor(part[0][:], prod[1][:, 0, :], prod[1][:, 1, :], ADD)
+        fetch(1, 3)
+        nc.vector.tensor_tensor(part[1][:], part[0][:], prod[1][:, 2, :], ADD)
+        nc.vector.tensor_tensor(result[0][:], pair[:, 0, :], pair[:, 1, :], ADD)
+        nc.sync.dma_start(out[0:P, :], result[0][:])
+        nc.vector.tensor_tensor(result[1][:], part[1][:], prod[1][:, 3, :], ADD)
+        nc.sync.dma_start(out[P : 2 * P, :], result[1][:])

@@ -41,19 +41,23 @@ def tile_picked_sub_lin_none_sub_e_kernel(tc, xT, w_words, w_scales, gate, offs,
         result = [keep.tile([P, V], F32, name=f"result{m}") for m in range(N // P)]
         warm = keep.tile([P, 2], F32, name="warm")
 
-        nc.sync.dma_start(offs_t[:], offs)
+        nc.vector.memset(w_bytes[:].bitcast(I32), 0)
+        for q in range(4):
+            nc.scalar.dma_start(w_bytes[32 * q : 32 * q + 4, :].bitcast(I32), w_scales[0, 4 * q : 4 * q + 4, :].bitcast(I32))
         x_rows = xT.rearrange("(p t) n -> p t n", t=PACK)
         for t in range(PACK):
             nc.sync.dma_start(planes[t][:], x_rows[:, t, :])
+            if t == 0:
+                nc.sync.dma_start(offs_t[:], offs)
         nc.sync.dma_start(w_codes[:].bitcast(I32), w_words[0].rearrange("p n r -> p (n r)").bitcast(I32))
-        nc.sync.dma_start(gates[0][:], gate[:, 0:P, :].rearrange("d p v -> p d v"))
-        for tile, source in zip(pos_t, (pos1, pos2, pos3, pos4)):
-            nc.sync.dma_start(tile[:], source)
+        nc.sync.dma_start(pos_t[0][:], pos1)
+        nc.sync.dma_start(gates[0][:, 0, :], gate[0, 0:P, :])
+        nc.sync.dma_start(pos_t[1][:], pos2)
+        nc.sync.dma_start(gates[0][:, 1:D, :], gate[1:D, 0:P, :].rearrange("d p v -> p d v"))
+        nc.sync.dma_start(pos_t[2][:], pos3)
+        nc.sync.dma_start(pos_t[3][:], pos4)
         nc.sync.dma_start(gates[1][:], gate[:, P : 2 * P, :].rearrange("d p v -> p d v"))
 
-        nc.vector.memset(w_bytes[:].bitcast(I32), 0)
-        for q in range(4):
-            nc.gpsimd.dma_start(w_bytes[32 * q : 32 * q + 4, :].bitcast(I32), w_scales[0, 4 * q : 4 * q + 4, :].bitcast(I32))
         nc.vector.memset(warm[:], 0.0)
         nc.scalar.copy(warm[:, 0:1], warm[:, 1:2])
 
@@ -68,24 +72,26 @@ def tile_picked_sub_lin_none_sub_e_kernel(tc, xT, w_words, w_scales, gate, offs,
                 out=x_codes[h][:].bitcast(FP8X4), scales=x_bytes[h][:], in_=picked[:, cols, :].rearrange("p n t -> p (n t)")
             )
 
-        for h in range(2):
-            for m in range(N // P):
-                rows = slice(m * P, (m + 1) * P)
-                acc = psum.tile([P, HALF], F32, name=f"acc{h}{m}")
-                nc.tensor.matmul_mx(
-                    out=acc[:],
-                    lhsT=w_codes[:, rows].bitcast(FP8X4),
-                    lhsT_scale=w_bytes[:, rows],
-                    rhs=x_codes[h][:].bitcast(FP8X4),
-                    rhs_scale=x_bytes[h][:],
-                    start=True,
-                    stop=True,
-                )
-                dst = y[m][:, h * HALF : (h + 1) * HALF]
-                if h == 0 and m == 0:
-                    nc.vector.tensor_copy(dst, acc[:])
-                else:
-                    nc.scalar.copy(dst, acc[:])
+        def multiply(m, h, first, width, engine_copy):
+            rows = slice(m * P, (m + 1) * P)
+            cols = slice(first, first + width)
+            acc = psum.tile([P, width], F32, name=f"acc{m}{h}{first}")
+            nc.tensor.matmul_mx(
+                out=acc[:],
+                lhsT=w_codes[:, rows].bitcast(FP8X4),
+                lhsT_scale=w_bytes[:, rows],
+                rhs=x_codes[h][:, cols].bitcast(FP8X4),
+                rhs_scale=x_bytes[h][:, cols],
+                start=True,
+                stop=True,
+            )
+            engine_copy(y[m][:, h * HALF + first : h * HALF + first + width], acc[:])
+
+        multiply(0, 0, 0, 256, nc.scalar.copy)
+        multiply(0, 1, 0, 128, nc.vector.tensor_copy)
+        multiply(0, 1, 128, 128, nc.scalar.copy)
+        multiply(1, 0, 0, 256, nc.scalar.copy)
+        multiply(1, 1, 0, 256, nc.scalar.copy)
 
         def fetch(m, d):
             nc.vector.tensor_tensor(prod[m][:, d, :], y[m][:].indirect(pos_t[d][:]), gates[m][:, d, :], MULT)

@@ -32,8 +32,8 @@ def tile_picked_sub_lin_none_sub_e_kernel(tc, xT, w_words, w_scales, gate, offs,
         w_bytes = keep.tile([P, N], U8, name="w_bytes", align_bytes=64)
         gates = [keep.tile([P, D, V], F32, name=f"gates{m}") for m in range(N // P)]
         picked = keep.tile([P, S, PACK], BF16, name="picked", align_bytes=64)
-        x_codes = [keep.tile([P, HALF], U32, name=f"x_codes{h}", align_bytes=64) for h in range(2)]
-        x_bytes = [keep.tile([P, HALF], U8, name=f"x_bytes{h}", align_bytes=64) for h in range(2)]
+        x_codes = keep.tile([P, S], U32, name="x_codes", align_bytes=64)
+        x_bytes = keep.tile([P, S], U8, name="x_bytes", align_bytes=64)
         y = [keep.tile([P, S], F32, name=f"y{m}") for m in range(N // P)]
         prod = [keep.tile([P, D, V], F32, name=f"prod{m}") for m in range(N // P)]
         pair = keep.tile([P, 2, V], F32, name="pair")
@@ -42,20 +42,18 @@ def tile_picked_sub_lin_none_sub_e_kernel(tc, xT, w_words, w_scales, gate, offs,
         warm = keep.tile([P, 2], F32, name="warm")
 
         nc.vector.memset(w_bytes[:].bitcast(I32), 0)
-        for q in range(4):
-            nc.scalar.dma_start(w_bytes[32 * q : 32 * q + 4, :].bitcast(I32), w_scales[0, 4 * q : 4 * q + 4, :].bitcast(I32))
         x_rows = xT.rearrange("(p t) n -> p t n", t=PACK)
         for t in range(PACK):
             nc.sync.dma_start(planes[t][:], x_rows[:, t, :])
             if t == 0:
                 nc.sync.dma_start(offs_t[:], offs)
+        for q in range(4):
+            nc.scalar.dma_start(w_bytes[32 * q : 32 * q + 4, :].bitcast(I32), w_scales[0, 4 * q : 4 * q + 4, :].bitcast(I32))
         nc.sync.dma_start(w_codes[:].bitcast(I32), w_words[0].rearrange("p n r -> p (n r)").bitcast(I32))
         nc.sync.dma_start(pos_t[0][:], pos1)
-        nc.sync.dma_start(gates[0][:, 0, :], gate[0, 0:P, :])
-        nc.sync.dma_start(pos_t[1][:], pos2)
-        nc.sync.dma_start(gates[0][:, 1:D, :], gate[1:D, 0:P, :].rearrange("d p v -> p d v"))
-        nc.sync.dma_start(pos_t[2][:], pos3)
-        nc.sync.dma_start(pos_t[3][:], pos4)
+        nc.sync.dma_start(gates[0][:], gate[:, 0:P, :].rearrange("d p v -> p d v"))
+        for tile, source in zip(pos_t[1:], (pos2, pos3, pos4)):
+            nc.sync.dma_start(tile[:], source)
         nc.sync.dma_start(gates[1][:], gate[:, P : 2 * P, :].rearrange("d p v -> p d v"))
 
         nc.vector.memset(warm[:], 0.0)
@@ -66,32 +64,35 @@ def tile_picked_sub_lin_none_sub_e_kernel(tc, xT, w_words, w_scales, gate, offs,
         for h in range(2):
             cols = slice(h * HALF, (h + 1) * HALF)
             nc.vector.tensor_copy(picked[:, cols, PACK - 1], planes[PACK - 1][:].indirect(offs_t[:, h * 16 : (h + 1) * 16]))
-        for h in range(2):
-            cols = slice(h * HALF, (h + 1) * HALF)
+        def quantise(first, width):
+            cols = slice(first, first + width)
             nc.vector.quantize_mx(
-                out=x_codes[h][:].bitcast(FP8X4), scales=x_bytes[h][:], in_=picked[:, cols, :].rearrange("p n t -> p (n t)")
+                out=x_codes[:, cols].bitcast(FP8X4), scales=x_bytes[:, cols], in_=picked[:, cols, :].rearrange("p n t -> p (n t)")
             )
 
-        def multiply(m, h, first, width, engine_copy):
+        def multiply(m, first, width, engine_copy):
             rows = slice(m * P, (m + 1) * P)
             cols = slice(first, first + width)
-            acc = psum.tile([P, width], F32, name=f"acc{m}{h}{first}")
+            acc = psum.tile([P, width], F32, name=f"acc{m}{first}")
             nc.tensor.matmul_mx(
                 out=acc[:],
                 lhsT=w_codes[:, rows].bitcast(FP8X4),
                 lhsT_scale=w_bytes[:, rows],
-                rhs=x_codes[h][:, cols].bitcast(FP8X4),
-                rhs_scale=x_bytes[h][:, cols],
+                rhs=x_codes[:, cols].bitcast(FP8X4),
+                rhs_scale=x_bytes[:, cols],
                 start=True,
                 stop=True,
             )
-            engine_copy(y[m][:, h * HALF + first : h * HALF + first + width], acc[:])
+            engine_copy(y[m][:, cols], acc[:])
 
-        multiply(0, 0, 0, 256, nc.scalar.copy)
-        multiply(0, 1, 0, 128, nc.vector.tensor_copy)
-        multiply(0, 1, 128, 128, nc.scalar.copy)
-        multiply(1, 0, 0, 256, nc.scalar.copy)
-        multiply(1, 1, 0, 256, nc.scalar.copy)
+        quantise(0, 256)
+        quantise(256, 128)
+        quantise(384, 128)
+        multiply(0, 0, 256, nc.scalar.copy)
+        multiply(0, 256, 128, nc.vector.tensor_copy)
+        multiply(0, 384, 128, nc.scalar.copy)
+        multiply(1, 0, 256, nc.scalar.copy)
+        multiply(1, 256, 256, nc.scalar.copy)
 
         def fetch(m, d):
             nc.vector.tensor_tensor(prod[m][:, d, :], y[m][:].indirect(pos_t[d][:]), gates[m][:, d, :], MULT)

from contextlib import ExitStack

import concourse.mybir as mybir

F32 = mybir.dt.float32
BF16 = mybir.dt.bfloat16
I32 = mybir.dt.int32
U32 = mybir.dt.uint32
U16 = mybir.dt.uint16
U8 = mybir.dt.uint8
FP8X4 = mybir.dt.float8_e4m3fn_x4
MULT = mybir.AluOpType.mult
ADD = mybir.AluOpType.add

P = 128
PACK = 4
K, T, S, D, V, N = 512, 2048, 512, 4, 256, 256
HALF = S // 2
FLOPS = 2 * K * S * N + 2 * D * N * V


def tile_picked_sub_lin_none_sub_e_kernel(tc, xT, w_words, w_scales, gate, offs, pos1, pos2, pos3, pos4, out):
    nc = tc.nc
    with ExitStack() as ctx:
        keep = ctx.enter_context(tc.tile_pool(name="keep", bufs=1))
        psum = ctx.enter_context(tc.psum_pool(name="psum", bufs=1))

        offs_t = keep.tile([P, S // 16], U16, name="offs_t")
        pos_t = [keep.tile([P, V // 16], U16, name=f"pos_t{d}") for d in range(D)]
        planes = [keep.tile([P, T], F32, name=f"plane{t}") for t in range(PACK)]
        w_codes = keep.tile([P, N], U32, name="w_codes", align_bytes=64)
        w_bytes = keep.tile([P, N], U8, name="w_bytes", align_bytes=64)
        gates = [keep.tile([P, D, V], F32, name=f"gates{m}") for m in range(N // P)]
        picked = keep.tile([P, S, PACK], BF16, name="picked", align_bytes=64)
        x_codes = keep.tile([P, S], U32, name="x_codes", align_bytes=64)
        x_bytes = keep.tile([P, S], U8, name="x_bytes", align_bytes=64)
        y = [keep.tile([P, S], F32, name=f"y{m}") for m in range(N // P)]
        prod = [keep.tile([P, D, V], F32, name=f"prod{m}") for m in range(N // P)]
        pair = keep.tile([P, 2, V], F32, name="pair")
        part = [keep.tile([P, V], F32, name=f"part{i}") for i in range(2)]
        result = [keep.tile([P, V], F32, name=f"result{m}") for m in range(N // P)]
        warm = keep.tile([P, 2], F32, name="warm")

        nc.vector.memset(w_bytes[:].bitcast(I32), 0)
        x_rows = xT.rearrange("(p t) n -> p t n", t=PACK)
        for t in range(PACK):
            nc.sync.dma_start(planes[t][:], x_rows[:, t, :])
            if t == 0:
                nc.sync.dma_start(offs_t[:], offs)
        for q in range(4):
            nc.scalar.dma_start(w_bytes[32 * q : 32 * q + 4, :].bitcast(I32), w_scales[0, 4 * q : 4 * q + 4, :].bitcast(I32))
        nc.sync.dma_start(w_codes[:].bitcast(I32), w_words[0].rearrange("p n r -> p (n r)").bitcast(I32))
        nc.sync.dma_start(pos_t[0][:], pos1)
        nc.sync.dma_start(gates[0][:], gate[:, 0:P, :].rearrange("d p v -> p d v"))
        for tile, source in zip(pos_t[1:], (pos2, pos3, pos4)):
            nc.sync.dma_start(tile[:], source)
        nc.sync.dma_start(gates[1][:], gate[:, P : 2 * P, :].rearrange("d p v -> p d v"))

        nc.vector.memset(warm[:], 0.0)
        nc.scalar.copy(warm[:, 0:1], warm[:, 1:2])

        for t in range(PACK - 1):
            nc.vector.tensor_copy(picked[:, :, t], planes[t][:].indirect(offs_t[:]))
        for h in range(2):
            cols = slice(h * HALF, (h + 1) * HALF)
            nc.vector.tensor_copy(picked[:, cols, PACK - 1], planes[PACK - 1][:].indirect(offs_t[:, h * 16 : (h + 1) * 16]))
        def quantise(first, width):
            cols = slice(first, first + width)
            nc.vector.quantize_mx(
                out=x_codes[:, cols].bitcast(FP8X4), scales=x_bytes[:, cols], in_=picked[:, cols, :].rearrange("p n t -> p (n t)")
            )

        def multiply(m, first, width, engine_copy):
            rows = slice(m * P, (m + 1) * P)
            cols = slice(first, first + width)
            acc = psum.tile([P, width], F32, name=f"acc{m}{first}")
            nc.tensor.matmul_mx(
                out=acc[:],
                lhsT=w_codes[:, rows].bitcast(FP8X4),
                lhsT_scale=w_bytes[:, rows],
                rhs=x_codes[:, cols].bitcast(FP8X4),
                rhs_scale=x_bytes[:, cols],
                start=True,
                stop=True,
            )
            engine_copy(y[m][:, cols], acc[:])

        quantise(0, 256)
        quantise(256, 128)
        quantise(384, 128)
        multiply(0, 0, 256, nc.scalar.copy)
        multiply(0, 256, 128, nc.vector.tensor_copy)
        multiply(0, 384, 128, nc.scalar.copy)
        multiply(1, 0, 256, nc.scalar.copy)
        multiply(1, 256, 256, nc.scalar.copy)

        def fetch(m, d):
            nc.vector.tensor_tensor(prod[m][:, d, :], y[m][:].indirect(pos_t[d][:]), gates[m][:, d, :], MULT)

        for d in range(D):
            fetch(0, d)
        fetch(1, 0)
        nc.vector.tensor_tensor(pair[:], prod[0][:, 0:2, :], prod[0][:, 2:4, :], ADD)
        fetch(1, 1)
        fetch(1, 2)
        nc.vector.tensor_tensor(part[0][:], prod[1][:, 0, :], prod[1][:, 1, :], ADD)
        fetch(1, 3)
        nc.vector.tensor_tensor(part[1][:], part[0][:], prod[1][:, 2, :], ADD)
        nc.vector.tensor_tensor(result[0][:], pair[:, 0, :], pair[:, 1, :], ADD)
        nc.sync.dma_start(out[0:P, :], result[0][:])
        nc.vector.tensor_tensor(result[1][:], part[1][:], prod[1][:, 3, :], ADD)
        nc.sync.dma_start(out[P : 2 * P, :], result[1][:])
